import numpy as np, ml_dtypes
CORES = [9,17,137,145,265,273,393,401]
N = 8
import mx_ref
NC, GR, GC, T = 256, 4, 2, 4
TA, TB = T // GC, T // GR
BF = ml_dtypes.bfloat16
def setup_inputs(rng):
    def f(*shape):
        return mx_ref.flush((rng.standard_normal(shape, dtype=np.float32) * np.exp2(rng.integers(-2, 3, shape[:-1] + (1,)))).astype(BF))
    return {"a": f(N, 128, TA * 512), "b": f(N, 128, TB * 4 * NC)}
def setup_inputs_blocks(rng):
    d = setup_inputs(rng)
    for k in ("a", "b"): d[k] = mx_ref.spread(d[k], rng, 1)
    return d
def setup_inputs_wide(rng):
    d = setup_inputs(rng)
    for k in ("a", "b"): d[k] = mx_ref.flush((d[k].astype(np.float32) * np.exp2(rng.integers(-8, 9, (N, 1, 1))).astype(np.float32)).astype(BF))
    return d
def setup_inputs_zeros(rng):
    d = setup_inputs(rng); v = d["b"].reshape(N, 128, -1, 4).copy()
    v[np.broadcast_to((rng.random((N, 1, v.shape[2], 1)) < 0.33), v.shape)] = 0
    d["b"] = v.reshape(d["b"].shape)
    return d
def reference(a, b):
    A = lambda i, s: mx_ref.quantize(a[i * GC + s // TA][:, 512 * (s % TA):512 * (s % TA) + 512])
    B = lambda s, j: mx_ref.quantize(b[(s // TB) * GC + j][:, 4 * NC * (s % TB):4 * NC * (s % TB) + 4 * NC])
    y = np.zeros((N, 128, NC), np.float32)
    for r in range(N):
        for s in range(T):
            p = mx_ref.matmul(A(r // GC, s), B(s, r % GC))
            y[r] = p if s == 0 else y[r] + p
    return {"y": y}

@@ -1,0 +1,161 @@
+from concourse.bass import DstId, RemoteDMATransfer
+from concourse.mybir import dt
+
+GR, GC = 4, 2
+WA, WB = 128, 256
+TA = 2
+SIM_CORES = 512
+
+RELAY_ON_OTHER_DIE = True
+
+SCRATCH = {
+    "abf": ("sbuf", [128, 4 * WA * TA], "bfloat16"),
+    "bbf": ("sbuf", [128, 4 * WB], "bfloat16"),
+    "aq": ("sbuf", [128, WA * GR], "float8_e4m3fn_x4"),
+    "ap": ("sbuf", [128, WA * GR], "uint8"),
+    "bq": ("sbuf", [128, WB * GR], "float8_e4m3fn_x4"),
+    "bp": ("sbuf", [128, WB * GR], "uint8"),
+    "ps": ("psum", [128, 512], "float32"),
+    "yo": ("sbuf", [128, WB], "float32"),
+}
+SEMAPHORES = (["lda", "ldb", "qa", "qb", "sent", "acod", "apln", "mm", "cp", "st"]
+              + ["bcod%d" % s for s in range(GR)] + ["bpln%d" % s for s in range(GR)])
+
+_CACHE = {}
+
+
+def _bits(mask):
+    return [e for e in range(mask.bit_length()) if (mask >> e) & 1]
+
+
+def _mask(engines):
+    return sum(1 << e for e in engines)
+
+
+def _plan(T, topo):
+    if "plan" in _CACHE:
+        return _CACHE["plan"]
+    cores = list(T.cores)
+    plan = {}
+    for r, c in enumerate(cores):
+        i, j = r // GC, r % GC
+        partner = cores[i * GC + (1 - j)]
+        far = near = None
+        for s in range(GR):
+            p = cores[s * GC + j]
+            if s == i or not topo.may_write(c, p):
+                continue
+            if topo.rack(topo.host(p)) == topo.rack(topo.host(c)):
+                near = s
+            else:
+                far = s
+        mine = [k for k in range(SIM_CORES)
+                if k != c and topo.host(k) == topo.host(c) and topo.chip(k) == topo.chip(c)
+                and topo.may_write(k, partner)]
+        mine.sort(key=lambda k: ((topo.die(k) == topo.die(c)) == RELAY_ON_OTHER_DIE, k))
+        rc, rp = mine[0], mine[1]
+        off = _bits(topo.mask(c, cores[far * GC + j]) & topo.mask(c, cores[near * GC + j]))
+        chip_only = [e for e in _bits(topo.mask(c, rc) & topo.mask(c, rp)) if e not in off]
+        plan[c] = ("rank", i, j, far, near, rc, rp, off, chip_only)
+        plan[rc] = ("relay", "aq", "acod", j, partner, len(chip_only))
+        plan[rp] = ("relay", "ap", "apln", j, partner, len(chip_only))
+    _CACHE["plan"] = plan
+    return plan
+
+
+def _view(T, name, c0, c1):
+    v = T[name][:, c0:c1]
+    return v.bitcast(dt.uint8) if name in ("aq", "bq") else v
+
+
+def _send(g, T, topo, core, dst, name, c0, c1, engines, sem):
+    rid, pid = topo.addr(dst, core)
+    g.remote_dma(_view(T, name, c0, c1), _view(T, name, c0, c1), sem, T.sem.sent, pid, rid, _mask(engines))
+    return len(engines)
+
+
+def _relay(g, core, T, topo, job):
+    _, name, sem, j, partner, n_in = job
+    c0, c1 = WA * TA * j, WA * TA * (j + 1)
+    g.wait_ge(T.sem[sem], n_in)
+    n = _send(g, T, topo, core, partner, name, c0, c1, _bits(topo.mask(core, partner)), T.sem[sem])
+    g.wait_ge(T.sem.sent, n)
+
+
+def _rank(g, core, T, topo, job):
+    _, i, j, far, near, rc, rp, off, chip_only = job
+    cores = list(T.cores)
+    c_far, c_near = cores[far * GC + j], cores[near * GC + j]
+    a0, a1 = WA * TA * j, WA * TA * (j + 1)
+    b0, b1 = WB * i, WB * (i + 1)
+    f0, f1 = WB * far, WB * (far + 1)
+    n_off = len(off)
+    half_far, half_near = off[1::2], off[0::2]
+
+    g.sync.dma_start(T.abf[:], T.a[:]).then_inc(T.sem.lda, 16)
+    g.sync.dma_start(T.bbf[:], T.b[:]).then_inc(T.sem.ldb, 16)
+
+    g.vector.wait_ge(T.sem.lda, 16)
+    for m in range(TA):
+        w = a0 + WA * m
+        g.vector.quantize_mx(T.aq[:, w:w + WA], T.ap[:, w:w + WA],
+                             T.abf[:, 4 * WA * m:4 * WA * (m + 1)]).then_inc(T.sem.qa, 1)
+    g.vector.wait_ge(T.sem.ldb, 16)
+    g.vector.quantize_mx(T.bq[:, b0:b1], T.bp[:, b0:b1], T.bbf[:]).then_inc(T.sem.qb, 1)
+
+    sent = 0
+    g.wait_ge(T.sem.qa, TA)
+    sent += _send(g, T, topo, core, rc, "aq", a0, a1, chip_only, T.sem.acod)
+    sent += _send(g, T, topo, core, rp, "ap", a0, a1, chip_only, T.sem.apln)
+    g.wait_ge(T.sem.qb, 1)
+    sent += _send(g, T, topo, core, c_far, "bq", b0, b1, off, T.sem["bcod%d" % i])
+    trs = []
+    for dst, eng in ((c_far, half_far), (c_near, half_near)):
+        rid, pid = topo.addr(dst, core)
+        trs.append(RemoteDMATransfer(dst_ids=[DstId(rid=rid, pnc=pid)], dma_engine_mask=_mask(eng),
+                                     remote_sem=T.sem["bpln%d" % i],
+                                     src=_view(T, "bp", b0, b1), dst=_view(T, "bp", b0, b1)))
+        sent += len(eng)
+    g.remote_dma_fused(trs, local_sem=T.sem.sent)
+    sent += _send(g, T, topo, core, c_near, "bq", b0, b1, off, T.sem["bcod%d" % i])
+    g.wait_ge(T.sem["bcod%d" % far], n_off)
+    sent += _send(g, T, topo, core, c_near, "bq", f0, f1, off, T.sem["bcod%d" % far])
+    g.wait_ge(T.sem["bpln%d" % far], len(half_far))
+    sent += _send(g, T, topo, core, c_near, "bp", f0, f1, off, T.sem["bpln%d" % far])
+
+    diag = [s for s in range(GR) if s not in (i, far, near)][0]
+    late = {i: 0, far: 1, near: 2, diag: 3}
+    plane_in = {far: len(half_far), near: len(half_near), diag: n_off}
+    order = sorted(range(GR), key=lambda s: (s // TA != j, late[s]))
+    t = g.tensor
+    t.wait_ge(T.sem.qa, TA)
+    t.wait_ge(T.sem.qb, 1)
+    got_a = False
+    for n, s in enumerate(order):
+        if s // TA != j and not got_a:
+            t.wait_ge(T.sem.acod, n_off)
+            t.wait_ge(T.sem.apln, n_off)
+            got_a = True
+        if s != i:
+            t.wait_ge(T.sem["bcod%d" % s], n_off)
+            t.wait_ge(T.sem["bpln%d" % s], plane_in[s])
+        t.matmul_mx(T.ps[:, 0:WB], T.aq[:, WA * s:WA * (s + 1)], T.ap[:, WA * s:WA * (s + 1)],
+                    T.bq[:, WB * s:WB * (s + 1)], T.bp[:, WB * s:WB * (s + 1)],
+                    n == 0, n == GR - 1).then_inc(T.sem.mm, 1)
+
+    g.vector.wait_ge(T.sem.mm, GR)
+    g.vector.tensor_copy(T.yo[:], T.ps[:, 0:WB]).then_inc(T.sem.cp, 1)
+    g.sync.wait_ge(T.sem.cp, 1)
+    g.sync.dma_start(T.y[:], T.yo[:]).then_inc(T.sem.st, 16)
+    g.sync.wait_ge(T.sem.st, 16)
+    g.wait_ge(T.sem.sent, sent)
+
+
+def rank_program(g, core, T, topo):
+    job = _plan(T, topo).get(core)
+    if job is None:
+        return
+    if job[0] == "relay":
+        _relay(g, core, T, topo, job)
+    else:
+        _rank(g, core, T, topo, job)

@@ -4,9 +4,9 @@ from concourse.mybir import dt
 GR, GC = 4, 2
 WA, WB = 128, 256
 TA = 2
+HB = WB // 2
+BANK = 512
 SIM_CORES = 512
-
-RELAY_ON_OTHER_DIE = True
 
 SCRATCH = {
     "abf": ("sbuf", [128, 4 * WA * TA], "bfloat16"),
@@ -15,11 +15,13 @@ SCRATCH = {
     "ap": ("sbuf", [128, WA * GR], "uint8"),
     "bq": ("sbuf", [128, WB * GR], "float8_e4m3fn_x4"),
     "bp": ("sbuf", [128, WB * GR], "uint8"),
-    "ps": ("psum", [128, 512], "float32"),
+    "ps": ("psum", [128, 2 * BANK], "float32"),
     "yo": ("sbuf", [128, WB], "float32"),
 }
-SEMAPHORES = (["lda", "ldb", "qa", "qb", "sent", "acod", "apln", "mm", "cp", "st"]
-              + ["bcod%d" % s for s in range(GR)] + ["bpln%d" % s for s in range(GR)])
+SEMAPHORES = (["lda0", "lda1", "ldb", "qa0", "qa1", "qb", "sent", "acod0", "acod1", "apln",
+               "mm0", "mm1", "cp0", "cp1", "st0", "st1"]
+              + ["bc0_%d" % s for s in range(GR)] + ["bc1_%d" % s for s in range(GR)]
+              + ["bpln%d" % s for s in range(GR)])
 
 _CACHE = {}
 
@@ -40,25 +42,29 @@ def _plan(T, topo):
     for r, c in enumerate(cores):
         i, j = r // GC, r % GC
         partner = cores[i * GC + (1 - j)]
-        far = near = None
+        far = near = diag = None
         for s in range(GR):
             p = cores[s * GC + j]
-            if s == i or not topo.may_write(c, p):
+            if s == i:
                 continue
-            if topo.rack(topo.host(p)) == topo.rack(topo.host(c)):
+            if not topo.may_write(c, p):
+                diag = s
+            elif topo.rack(topo.host(p)) == topo.rack(topo.host(c)):
                 near = s
             else:
                 far = s
+        late = {i: 0, far: 1, near: 2, diag: 3}
         mine = [k for k in range(SIM_CORES)
                 if k != c and topo.host(k) == topo.host(c) and topo.chip(k) == topo.chip(c)
-                and topo.may_write(k, partner)]
-        mine.sort(key=lambda k: ((topo.die(k) == topo.die(c)) == RELAY_ON_OTHER_DIE, k))
+                and topo.may_write(k, partner) and topo.die(k) != topo.die(c)]
         rc, rp = mine[0], mine[1]
         off = _bits(topo.mask(c, cores[far * GC + j]) & topo.mask(c, cores[near * GC + j]))
         chip_only = [e for e in _bits(topo.mask(c, rc) & topo.mask(c, rp)) if e not in off]
-        plan[c] = ("rank", i, j, far, near, rc, rp, off, chip_only)
-        plan[rc] = ("relay", "aq", "acod", j, partner, len(chip_only))
-        plan[rp] = ("relay", "ap", "apln", j, partner, len(chip_only))
+        plan[c] = ("rank", i, j, far, near, late, rc, rp, off, chip_only)
+        tiles = sorted(range(TA * j, TA * (j + 1)), key=lambda s: late[s])
+        plan[rc] = ("relay", "aq", partner, len(chip_only),
+                    [("acod%d" % k, WA * s, WA * (s + 1)) for k, s in enumerate(tiles)])
+        plan[rp] = ("relay", "ap", partner, len(chip_only), [("apln", WA * TA * j, WA * TA * (j + 1))])
     _CACHE["plan"] = plan
     return plan
 
@@ -70,45 +76,53 @@ def _view(T, name, c0, c1):
 
 def _send(g, T, topo, core, dst, name, c0, c1, engines, sem):
     rid, pid = topo.addr(dst, core)
-    g.remote_dma(_view(T, name, c0, c1), _view(T, name, c0, c1), sem, T.sem.sent, pid, rid, _mask(engines))
+    g.remote_dma(_view(T, name, c0, c1), _view(T, name, c0, c1), T.sem[sem], T.sem.sent, pid, rid, _mask(engines))
     return len(engines)
 
 
 def _relay(g, core, T, topo, job):
-    _, name, sem, j, partner, n_in = job
-    c0, c1 = WA * TA * j, WA * TA * (j + 1)
-    g.wait_ge(T.sem[sem], n_in)
-    n = _send(g, T, topo, core, partner, name, c0, c1, _bits(topo.mask(core, partner)), T.sem[sem])
+    _, name, partner, n_in, pieces = job
+    n = 0
+    for sem, c0, c1 in pieces:
+        g.wait_ge(T.sem[sem], n_in)
+        n += _send(g, T, topo, core, partner, name, c0, c1, _bits(topo.mask(core, partner)), sem)
     g.wait_ge(T.sem.sent, n)
 
 
 def _rank(g, core, T, topo, job):
-    _, i, j, far, near, rc, rp, off, chip_only = job
+    _, i, j, far, near, late, rc, rp, off, chip_only = job
     cores = list(T.cores)
     c_far, c_near = cores[far * GC + j], cores[near * GC + j]
-    a0, a1 = WA * TA * j, WA * TA * (j + 1)
     b0, b1 = WB * i, WB * (i + 1)
     f0, f1 = WB * far, WB * (far + 1)
     n_off = len(off)
     half_far, half_near = off[1::2], off[0::2]
+    own = sorted(range(TA * j, TA * (j + 1)), key=lambda s: late[s])
+    theirs = sorted(range(TA * (1 - j), TA * (2 - j)), key=lambda s: late[s])
 
-    g.sync.dma_start(T.abf[:], T.a[:]).then_inc(T.sem.lda, 16)
+    for k, (s, q) in enumerate(zip(own, (g.sync, g.scalar))):
+        m = s - TA * j
+        q.dma_start(T.abf[:, 4 * WA * m:4 * WA * (m + 1)], T.a[:, 4 * WA * m:4 * WA * (m + 1)]).then_inc(
+            T.sem["lda%d" % k], 16)
     g.sync.dma_start(T.bbf[:], T.b[:]).then_inc(T.sem.ldb, 16)
 
-    g.vector.wait_ge(T.sem.lda, 16)
-    for m in range(TA):
-        w = a0 + WA * m
-        g.vector.quantize_mx(T.aq[:, w:w + WA], T.ap[:, w:w + WA],
-                             T.abf[:, 4 * WA * m:4 * WA * (m + 1)]).then_inc(T.sem.qa, 1)
+    for k, s in enumerate(own):
+        m = s - TA * j
+        g.vector.wait_ge(T.sem["lda%d" % k], 16)
+        g.vector.quantize_mx(T.aq[:, WA * s:WA * (s + 1)], T.ap[:, WA * s:WA * (s + 1)],
+                             T.abf[:, 4 * WA * m:4 * WA * (m + 1)]).then_inc(T.sem["qa%d" % k], 1)
     g.vector.wait_ge(T.sem.ldb, 16)
     g.vector.quantize_mx(T.bq[:, b0:b1], T.bp[:, b0:b1], T.bbf[:]).then_inc(T.sem.qb, 1)
 
     sent = 0
-    g.wait_ge(T.sem.qa, TA)
-    sent += _send(g, T, topo, core, rc, "aq", a0, a1, chip_only, T.sem.acod)
-    sent += _send(g, T, topo, core, rp, "ap", a0, a1, chip_only, T.sem.apln)
+    g.wait_ge(T.sem.qa0, 1)
+    sent += _send(g, T, topo, core, rc, "aq", WA * own[0], WA * (own[0] + 1), chip_only, "acod0")
+    g.wait_ge(T.sem.qa1, 1)
+    sent += _send(g, T, topo, core, rp, "ap", WA * TA * j, WA * TA * (j + 1), chip_only, "apln")
     g.wait_ge(T.sem.qb, 1)
-    sent += _send(g, T, topo, core, c_far, "bq", b0, b1, off, T.sem["bcod%d" % i])
+    sent += _send(g, T, topo, core, c_far, "bq", b0, b0 + HB, off, "bc0_%d" % i)
+    sent += _send(g, T, topo, core, c_far, "bq", b0 + HB, b1, off, "bc1_%d" % i)
+    sent += _send(g, T, topo, core, rc, "aq", WA * own[1], WA * (own[1] + 1), chip_only, "acod1")
     trs = []
     for dst, eng in ((c_far, half_far), (c_near, half_near)):
         rid, pid = topo.addr(dst, core)
@@ -117,37 +131,42 @@ def _rank(g, core, T, topo, job):
                                      src=_view(T, "bp", b0, b1), dst=_view(T, "bp", b0, b1)))
         sent += len(eng)
     g.remote_dma_fused(trs, local_sem=T.sem.sent)
-    sent += _send(g, T, topo, core, c_near, "bq", b0, b1, off, T.sem["bcod%d" % i])
-    g.wait_ge(T.sem["bcod%d" % far], n_off)
-    sent += _send(g, T, topo, core, c_near, "bq", f0, f1, off, T.sem["bcod%d" % far])
-    g.wait_ge(T.sem["bpln%d" % far], len(half_far))
-    sent += _send(g, T, topo, core, c_near, "bp", f0, f1, off, T.sem["bpln%d" % far])
+    sent += _send(g, T, topo, core, c_near, "bq", b0, b1, off, "bc0_%d" % i)
+    for name, c0, c1, sem, n_in in (("bq", f0, f0 + HB, "bc0_%d" % far, n_off),
+                                    ("bq", f0 + HB, f1, "bc1_%d" % far, n_off),
+                                    ("bp", f0, f1, "bpln%d" % far, len(half_far))):
+        g.wait_ge(T.sem[sem], n_in)
+        sent += _send(g, T, topo, core, c_near, name, c0, c1, off, sem)
 
-    diag = [s for s in range(GR) if s not in (i, far, near)][0]
-    late = {i: 0, far: 1, near: 2, diag: 3}
-    plane_in = {far: len(half_far), near: len(half_near), diag: n_off}
-    order = sorted(range(GR), key=lambda s: (s // TA != j, late[s]))
+    plane_in = {far: len(half_far), near: len(half_near)}
+    when = {s: late[s] for s in own}
+    when[theirs[0]], when[theirs[1]] = 2.5, 3.5
     t = g.tensor
-    t.wait_ge(T.sem.qa, TA)
+    t.wait_ge(T.sem.qa0, 1)
+    t.wait_ge(T.sem.qa1, 1)
     t.wait_ge(T.sem.qb, 1)
-    got_a = False
-    for n, s in enumerate(order):
-        if s // TA != j and not got_a:
-            t.wait_ge(T.sem.acod, n_off)
-            t.wait_ge(T.sem.apln, n_off)
-            got_a = True
+    for n, s in enumerate(sorted(range(GR), key=lambda s: when[s])):
         if s != i:
-            t.wait_ge(T.sem["bcod%d" % s], n_off)
-            t.wait_ge(T.sem["bpln%d" % s], plane_in[s])
-        t.matmul_mx(T.ps[:, 0:WB], T.aq[:, WA * s:WA * (s + 1)], T.ap[:, WA * s:WA * (s + 1)],
-                    T.bq[:, WB * s:WB * (s + 1)], T.bp[:, WB * s:WB * (s + 1)],
-                    n == 0, n == GR - 1).then_inc(T.sem.mm, 1)
+            t.wait_ge(T.sem["bc0_%d" % s], n_off)
+            if s != near:
+                t.wait_ge(T.sem["bc1_%d" % s], n_off)
+            t.wait_ge(T.sem["bpln%d" % s], plane_in.get(s, n_off))
+        if s in theirs:
+            t.wait_ge(T.sem.apln, n_off)
+            t.wait_ge(T.sem["acod%d" % theirs.index(s)], n_off)
+        for h in range(2):
+            c0 = WB * s + HB * h
+            t.matmul_mx(T.ps[:, BANK * h:BANK * h + HB], T.aq[:, WA * s:WA * (s + 1)], T.ap[:, WA * s:WA * (s + 1)],
+                        T.bq[:, c0:c0 + HB], T.bp[:, c0:c0 + HB],
+                        n == 0, n == GR - 1).then_inc(T.sem["mm%d" % h], 1)
 
-    g.vector.wait_ge(T.sem.mm, GR)
-    g.vector.tensor_copy(T.yo[:], T.ps[:, 0:WB]).then_inc(T.sem.cp, 1)
-    g.sync.wait_ge(T.sem.cp, 1)
-    g.sync.dma_start(T.y[:], T.yo[:]).then_inc(T.sem.st, 16)
-    g.sync.wait_ge(T.sem.st, 16)
+    for h, q in enumerate((g.sync, g.scalar)):
+        g.vector.wait_ge(T.sem["mm%d" % h], GR)
+        g.vector.tensor_copy(T.yo[:, HB * h:HB * (h + 1)],
+                             T.ps[:, BANK * h:BANK * h + HB]).then_inc(T.sem["cp%d" % h], 1)
+        q.wait_ge(T.sem["cp%d" % h], 1)
+        q.dma_start(T.y[:, HB * h:HB * (h + 1)], T.yo[:, HB * h:HB * (h + 1)]).then_inc(T.sem["st%d" % h], 16)
+        q.wait_ge(T.sem["st%d" % h], 16)
     g.wait_ge(T.sem.sent, sent)
 
 

@@ -18,7 +18,7 @@ SCRATCH = {
     "ps": ("psum", [128, 2 * BANK], "float32"),
     "yo": ("sbuf", [128, WB], "float32"),
 }
-SEMAPHORES = (["lda0", "lda1", "ldb", "qa0", "qa1", "qb", "sent", "acod0", "acod1", "apln",
+SEMAPHORES = (["lda0", "lda1", "ldb0", "ldb1", "qa0", "qa1", "qb0", "qb1", "sent", "acod0", "acod1", "apln",
                "mm0", "mm1", "cp0", "cp1", "st0", "st1"]
               + ["bc0_%d" % s for s in range(GR)] + ["bc1_%d" % s for s in range(GR)]
               + ["bpln%d" % s for s in range(GR)])
@@ -53,18 +53,30 @@ def _plan(T, topo):
                 near = s
             else:
                 far = s
-        late = {i: 0, far: 1, near: 2, diag: 3}
-        mine = [k for k in range(SIM_CORES)
-                if k != c and topo.host(k) == topo.host(c) and topo.chip(k) == topo.chip(c)
-                and topo.may_write(k, partner) and topo.die(k) != topo.die(c)]
-        rc, rp = mine[0], mine[1]
-        off = _bits(topo.mask(c, cores[far * GC + j]) & topo.mask(c, cores[near * GC + j]))
-        chip_only = [e for e in _bits(topo.mask(c, rc) & topo.mask(c, rp)) if e not in off]
-        plan[c] = ("rank", i, j, far, near, late, rc, rp, off, chip_only)
+        late = {i: 0, far: 1, near: 2.5, diag: 3}
+        chipmates = [k for k in range(SIM_CORES)
+                     if k != c and topo.host(k) == topo.host(c) and topo.chip(k) == topo.chip(c)]
+        mine = [k for k in chipmates if topo.may_write(k, partner)]
+        there = [k for k in mine if topo.die(k) != topo.die(c)]
+        here = [k for k in mine if topo.die(k) == topo.die(c)]
+        rc = [there[0], here[0]]
+        rp = there[1]
+        c_far, c_near = cores[far * GC + j], cores[near * GC + j]
+        free = [k for k in chipmates if k not in rc and k != rp and topo.may_write(k, c_near)
+                and topo.may_write(k, c_far)]
+        hb = [k for k in free if topo.die(k) != topo.die(c)][:2]
+        hp = [k for k in free if topo.die(k) == topo.die(c)][0]
+        off = _bits(topo.mask(c, c_far) & topo.mask(c, c_near))
+        chip_only = [e for e in _bits(topo.mask(c, rc[0])) if e not in off]
+        n_in = len(chip_only) // 2
+        plan[c] = ("rank", i, j, far, near, late, rc, rp, hb, hp, off, chip_only)
         tiles = sorted(range(TA * j, TA * (j + 1)), key=lambda s: late[s])
-        plan[rc] = ("relay", "aq", partner, len(chip_only),
-                    [("acod%d" % k, WA * s, WA * (s + 1)) for k, s in enumerate(tiles)])
-        plan[rp] = ("relay", "ap", partner, len(chip_only), [("apln", WA * TA * j, WA * TA * (j + 1))])
+        for k, s in enumerate(tiles):
+            plan[rc[k]] = ("relay", "aq", [partner], n_in, "acod%d" % k, WA * s, WA * (s + 1))
+        plan[rp] = ("relay", "ap", [partner], n_in, "apln", WA * TA * j, WA * TA * (j + 1))
+        plan[hb[0]] = ("relay", "bq", [c_near], n_in, "bc0_%d" % i, WB * i, WB * i + HB)
+        plan[hb[1]] = ("relay", "bq", [c_far, c_near], n_in, "bc1_%d" % i, WB * i + HB, WB * (i + 1))
+        plan[hp] = ("relay", "bp", [c_near], n_in, "bpln%d" % i, WB * i, WB * (i + 1))
     _CACHE["plan"] = plan
     return plan
 
@@ -80,81 +92,90 @@ def _send(g, T, topo, core, dst, name, c0, c1, engines, sem):
     return len(engines)
 
 
+def _fused(g, T, topo, core, parts):
+    trs, n = [], 0
+    for dst, name, c0, c1, eng, sem in parts:
+        rid, pid = topo.addr(dst, core)
+        trs.append(RemoteDMATransfer(dst_ids=[DstId(rid=rid, pnc=pid)], dma_engine_mask=_mask(eng),
+                                     remote_sem=T.sem[sem],
+                                     src=_view(T, name, c0, c1), dst=_view(T, name, c0, c1)))
+        n += len(eng)
+    g.remote_dma_fused(trs, local_sem=T.sem.sent)
+    return n
+
+
 def _relay(g, core, T, topo, job):
-    _, name, partner, n_in, pieces = job
+    _, name, dsts, n_in, sem, c0, c1 = job
+    g.wait_ge(T.sem[sem], n_in)
     n = 0
-    for sem, c0, c1 in pieces:
-        g.wait_ge(T.sem[sem], n_in)
-        n += _send(g, T, topo, core, partner, name, c0, c1, _bits(topo.mask(core, partner)), sem)
+    for dst in dsts:
+        n += _send(g, T, topo, core, dst, name, c0, c1, _bits(topo.mask(core, dst))[0::2], sem)
     g.wait_ge(T.sem.sent, n)
 
 
 def _rank(g, core, T, topo, job):
-    _, i, j, far, near, late, rc, rp, off, chip_only = job
+    _, i, j, far, near, late, rc, rp, hb, hp, off, chip_only = job
     cores = list(T.cores)
     c_far, c_near = cores[far * GC + j], cores[near * GC + j]
     b0, b1 = WB * i, WB * (i + 1)
     f0, f1 = WB * far, WB * (far + 1)
     n_off = len(off)
-    half_far, half_near = off[1::2], off[0::2]
+    n_rel = len(off[0::2])
     own = sorted(range(TA * j, TA * (j + 1)), key=lambda s: late[s])
     theirs = sorted(range(TA * (1 - j), TA * (2 - j)), key=lambda s: late[s])
 
-    for k, (s, q) in enumerate(zip(own, (g.sync, g.scalar))):
-        m = s - TA * j
-        q.dma_start(T.abf[:, 4 * WA * m:4 * WA * (m + 1)], T.a[:, 4 * WA * m:4 * WA * (m + 1)]).then_inc(
-            T.sem["lda%d" % k], 16)
-    g.sync.dma_start(T.bbf[:], T.b[:]).then_inc(T.sem.ldb, 16)
+    for kind, k, q in (("b", 1, g.sync), ("a", 0, g.scalar), ("b", 0, g.sync), ("a", 1, g.scalar)):
+        if kind == "a":
+            m = own[k] - TA * j
+            q.dma_start(T.abf[:, 4 * WA * m:4 * WA * (m + 1)], T.a[:, 4 * WA * m:4 * WA * (m + 1)]).then_inc(
+                T.sem["lda%d" % k], 16)
+        else:
+            q.dma_start(T.bbf[:, 4 * HB * k:4 * HB * (k + 1)], T.b[:, 4 * HB * k:4 * HB * (k + 1)]).then_inc(
+                T.sem["ldb%d" % k], 16)
+    for kind, k in (("b", 1), ("a", 0), ("b", 0), ("a", 1)):
+        g.vector.wait_ge(T.sem["ld%s%d" % (kind, k)], 16)
+        if kind == "a":
+            s = own[k]
+            m = s - TA * j
+            g.vector.quantize_mx(T.aq[:, WA * s:WA * (s + 1)], T.ap[:, WA * s:WA * (s + 1)],
+                                 T.abf[:, 4 * WA * m:4 * WA * (m + 1)]).then_inc(T.sem["qa%d" % k], 1)
+        else:
+            g.vector.quantize_mx(T.bq[:, b0 + HB * k:b0 + HB * (k + 1)], T.bp[:, b0 + HB * k:b0 + HB * (k + 1)],
+                                 T.bbf[:, 4 * HB * k:4 * HB * (k + 1)]).then_inc(T.sem["qb%d" % k], 1)
 
-    for k, s in enumerate(own):
-        m = s - TA * j
-        g.vector.wait_ge(T.sem["lda%d" % k], 16)
-        g.vector.quantize_mx(T.aq[:, WA * s:WA * (s + 1)], T.ap[:, WA * s:WA * (s + 1)],
-                             T.abf[:, 4 * WA * m:4 * WA * (m + 1)]).then_inc(T.sem["qa%d" % k], 1)
-    g.vector.wait_ge(T.sem.ldb, 16)
-    g.vector.quantize_mx(T.bq[:, b0:b1], T.bp[:, b0:b1], T.bbf[:]).then_inc(T.sem.qb, 1)
-
+    ev, od = chip_only[0::2], chip_only[1::2]
     sent = 0
+    g.wait_ge(T.sem.qb1, 1)
+    sent += _send(g, T, topo, core, hb[1], "bq", b0 + HB, b1, ev, "bc1_%d" % i)
     g.wait_ge(T.sem.qa0, 1)
-    sent += _send(g, T, topo, core, rc, "aq", WA * own[0], WA * (own[0] + 1), chip_only, "acod0")
+    sent += _send(g, T, topo, core, rc[0], "aq", WA * own[0], WA * (own[0] + 1), od, "acod0")
+    g.wait_ge(T.sem.qb0, 1)
     g.wait_ge(T.sem.qa1, 1)
-    sent += _send(g, T, topo, core, rp, "ap", WA * TA * j, WA * TA * (j + 1), chip_only, "apln")
-    g.wait_ge(T.sem.qb, 1)
-    sent += _send(g, T, topo, core, c_far, "bq", b0, b0 + HB, off, "bc0_%d" % i)
-    sent += _send(g, T, topo, core, c_far, "bq", b0 + HB, b1, off, "bc1_%d" % i)
-    sent += _send(g, T, topo, core, rc, "aq", WA * own[1], WA * (own[1] + 1), chip_only, "acod1")
-    trs = []
-    for dst, eng in ((c_far, half_far), (c_near, half_near)):
-        rid, pid = topo.addr(dst, core)
-        trs.append(RemoteDMATransfer(dst_ids=[DstId(rid=rid, pnc=pid)], dma_engine_mask=_mask(eng),
-                                     remote_sem=T.sem["bpln%d" % i],
-                                     src=_view(T, "bp", b0, b1), dst=_view(T, "bp", b0, b1)))
-        sent += len(eng)
-    g.remote_dma_fused(trs, local_sem=T.sem.sent)
-    sent += _send(g, T, topo, core, c_near, "bq", b0, b1, off, "bc0_%d" % i)
-    for name, c0, c1, sem, n_in in (("bq", f0, f0 + HB, "bc0_%d" % far, n_off),
-                                    ("bq", f0 + HB, f1, "bc1_%d" % far, n_off),
-                                    ("bp", f0, f1, "bpln%d" % far, len(half_far))):
+    sent += _fused(g, T, topo, core, [(c_far, "bq", b0, b0 + HB, off, "bc0_%d" % i),
+                                      (rc[1], "aq", WA * own[1], WA * (own[1] + 1), ev, "acod1"),
+                                      (hb[0], "bq", b0, b0 + HB, od, "bc0_%d" % i)])
+    sent += _fused(g, T, topo, core, [(c_far, "bp", b0, b1, off, "bpln%d" % i),
+                                      (rp, "ap", WA * TA * j, WA * TA * (j + 1), ev, "apln"),
+                                      (hp, "bp", b0, b1, od, "bpln%d" % i)])
+    for name, c0, c1, sem, n_in in (("bq", f0, f0 + HB, "bc0_%d" % far, n_off), ("bp", f0, f1, "bpln%d" % far, n_off),
+                                    ("bq", f0 + HB, f1, "bc1_%d" % far, n_rel)):
         g.wait_ge(T.sem[sem], n_in)
         sent += _send(g, T, topo, core, c_near, name, c0, c1, off, sem)
 
-    plane_in = {far: len(half_far), near: len(half_near)}
-    when = {s: late[s] for s in own}
-    when[theirs[0]], when[theirs[1]] = 2.5, 3.5
+    when = {s: max(late[s], 2 if s in theirs else 0) for s in range(GR)}
     t = g.tensor
     t.wait_ge(T.sem.qa0, 1)
     t.wait_ge(T.sem.qa1, 1)
-    t.wait_ge(T.sem.qb, 1)
+    t.wait_ge(T.sem.qb0, 1)
+    t.wait_ge(T.sem.qb1, 1)
     for n, s in enumerate(sorted(range(GR), key=lambda s: when[s])):
-        if s != i:
-            t.wait_ge(T.sem["bc0_%d" % s], n_off)
-            if s != near:
-                t.wait_ge(T.sem["bc1_%d" % s], n_off)
-            t.wait_ge(T.sem["bpln%d" % s], plane_in.get(s, n_off))
         if s in theirs:
-            t.wait_ge(T.sem.apln, n_off)
-            t.wait_ge(T.sem["acod%d" % theirs.index(s)], n_off)
+            t.wait_ge(T.sem.apln, n_rel)
+            t.wait_ge(T.sem["acod%d" % theirs.index(s)], n_rel)
         for h in range(2):
+            if s != i:
+                t.wait_ge(T.sem["bc%d_%d" % (h, s)], n_rel if s == near or (s == far and h == 1) else n_off)
+                t.wait_ge(T.sem["bpln%d" % s], n_rel if s == near else n_off)
             c0 = WB * s + HB * h
             t.matmul_mx(T.ps[:, BANK * h:BANK * h + HB], T.aq[:, WA * s:WA * (s + 1)], T.ap[:, WA * s:WA * (s + 1)],
                         T.bq[:, c0:c0 + HB], T.bp[:, c0:c0 + HB],

from concourse.bass import DstId, RemoteDMATransfer
from concourse.mybir import dt

GR, GC = 4, 2
WA, WB = 128, 256
TA = 2
HB = WB // 2
BANK = 512
SIM_CORES = 512

SCRATCH = {
    "abf": ("sbuf", [128, 4 * WA * TA], "bfloat16"),
    "bbf": ("sbuf", [128, 4 * WB], "bfloat16"),
    "aq": ("sbuf", [128, WA * GR], "float8_e4m3fn_x4"),
    "ap": ("sbuf", [128, WA * GR], "uint8"),
    "bq": ("sbuf", [128, WB * GR], "float8_e4m3fn_x4"),
    "bp": ("sbuf", [128, WB * GR], "uint8"),
    "ps": ("psum", [128, 2 * BANK], "float32"),
    "yo": ("sbuf", [128, WB], "float32"),
}
SEMAPHORES = (["lda0", "lda1", "ldb0", "ldb1", "qa0", "qa1", "qb0", "qb1", "sent", "acod0", "acod1", "apln",
               "mm0", "mm1", "cp0", "cp1", "st0", "st1"]
              + ["bc0_%d" % s for s in range(GR)] + ["bc1_%d" % s for s in range(GR)]
              + ["bpln%d" % s for s in range(GR)])

_CACHE = {}


def _bits(mask):
    return [e for e in range(mask.bit_length()) if (mask >> e) & 1]


def _mask(engines):
    return sum(1 << e for e in engines)


def _plan(T, topo):
    if "plan" in _CACHE:
        return _CACHE["plan"]
    cores = list(T.cores)
    plan = {}
    for r, c in enumerate(cores):
        i, j = r // GC, r % GC
        partner = cores[i * GC + (1 - j)]
        far = near = diag = None
        for s in range(GR):
            p = cores[s * GC + j]
            if s == i:
                continue
            if not topo.may_write(c, p):
                diag = s
            elif topo.rack(topo.host(p)) == topo.rack(topo.host(c)):
                near = s
            else:
                far = s
        late = {i: 0, far: 1, near: 2.5, diag: 3}
        chipmates = [k for k in range(SIM_CORES)
                     if k != c and topo.host(k) == topo.host(c) and topo.chip(k) == topo.chip(c)]
        mine = [k for k in chipmates if topo.may_write(k, partner)]
        there = [k for k in mine if topo.die(k) != topo.die(c)]
        here = [k for k in mine if topo.die(k) == topo.die(c)]
        rc = [there[0], here[0]]
        rp = there[1]
        c_far, c_near = cores[far * GC + j], cores[near * GC + j]
        free = [k for k in chipmates if k not in rc and k != rp and topo.may_write(k, c_near)
                and topo.may_write(k, c_far)]
        hb = [k for k in free if topo.die(k) != topo.die(c)][:2]
        hp = [k for k in free if topo.die(k) == topo.die(c)][0]
        off = _bits(topo.mask(c, c_far) & topo.mask(c, c_near))
        chip_only = [e for e in _bits(topo.mask(c, rc[0])) if e not in off]
        n_in = len(chip_only) // 2
        plan[c] = ("rank", i, j, far, near, late, rc, rp, hb, hp, off, chip_only)
        tiles = sorted(range(TA * j, TA * (j + 1)), key=lambda s: late[s])
        for k, s in enumerate(tiles):
            plan[rc[k]] = ("relay", "aq", [partner], n_in, "acod%d" % k, WA * s, WA * (s + 1))
        plan[rp] = ("relay", "ap", [partner], n_in, "apln", WA * TA * j, WA * TA * (j + 1))
        plan[hb[0]] = ("relay", "bq", [c_near], n_in, "bc0_%d" % i, WB * i, WB * i + HB)
        plan[hb[1]] = ("relay", "bq", [c_far, c_near], n_in, "bc1_%d" % i, WB * i + HB, WB * (i + 1))
        plan[hp] = ("relay", "bp", [c_near], n_in, "bpln%d" % i, WB * i, WB * (i + 1))
    _CACHE["plan"] = plan
    return plan


def _view(T, name, c0, c1):
    v = T[name][:, c0:c1]
    return v.bitcast(dt.uint8) if name in ("aq", "bq") else v


def _send(g, T, topo, core, dst, name, c0, c1, engines, sem):
    rid, pid = topo.addr(dst, core)
    g.remote_dma(_view(T, name, c0, c1), _view(T, name, c0, c1), T.sem[sem], T.sem.sent, pid, rid, _mask(engines))
    return len(engines)


def _fused(g, T, topo, core, parts):
    trs, n = [], 0
    for dst, name, c0, c1, eng, sem in parts:
        rid, pid = topo.addr(dst, core)
        trs.append(RemoteDMATransfer(dst_ids=[DstId(rid=rid, pnc=pid)], dma_engine_mask=_mask(eng),
                                     remote_sem=T.sem[sem],
                                     src=_view(T, name, c0, c1), dst=_view(T, name, c0, c1)))
        n += len(eng)
    g.remote_dma_fused(trs, local_sem=T.sem.sent)
    return n


def _relay(g, core, T, topo, job):
    _, name, dsts, n_in, sem, c0, c1 = job
    g.wait_ge(T.sem[sem], n_in)
    n = 0
    for dst in dsts:
        n += _send(g, T, topo, core, dst, name, c0, c1, _bits(topo.mask(core, dst))[0::2], sem)
    g.wait_ge(T.sem.sent, n)


def _rank(g, core, T, topo, job):
    _, i, j, far, near, late, rc, rp, hb, hp, off, chip_only = job
    cores = list(T.cores)
    c_far, c_near = cores[far * GC + j], cores[near * GC + j]
    b0, b1 = WB * i, WB * (i + 1)
    f0, f1 = WB * far, WB * (far + 1)
    n_off = len(off)
    n_rel = len(off[0::2])
    own = sorted(range(TA * j, TA * (j + 1)), key=lambda s: late[s])
    theirs = sorted(range(TA * (1 - j), TA * (2 - j)), key=lambda s: late[s])

    for kind, k, q in (("b", 1, g.sync), ("a", 0, g.scalar), ("b", 0, g.sync), ("a", 1, g.scalar)):
        if kind == "a":
            m = own[k] - TA * j
            q.dma_start(T.abf[:, 4 * WA * m:4 * WA * (m + 1)], T.a[:, 4 * WA * m:4 * WA * (m + 1)]).then_inc(
                T.sem["lda%d" % k], 16)
        else:
            q.dma_start(T.bbf[:, 4 * HB * k:4 * HB * (k + 1)], T.b[:, 4 * HB * k:4 * HB * (k + 1)]).then_inc(
                T.sem["ldb%d" % k], 16)
    for kind, k in (("b", 1), ("a", 0), ("b", 0), ("a", 1)):
        g.vector.wait_ge(T.sem["ld%s%d" % (kind, k)], 16)
        if kind == "a":
            s = own[k]
            m = s - TA * j
            g.vector.quantize_mx(T.aq[:, WA * s:WA * (s + 1)], T.ap[:, WA * s:WA * (s + 1)],
                                 T.abf[:, 4 * WA * m:4 * WA * (m + 1)]).then_inc(T.sem["qa%d" % k], 1)
        else:
            g.vector.quantize_mx(T.bq[:, b0 + HB * k:b0 + HB * (k + 1)], T.bp[:, b0 + HB * k:b0 + HB * (k + 1)],
                                 T.bbf[:, 4 * HB * k:4 * HB * (k + 1)]).then_inc(T.sem["qb%d" % k], 1)

    ev, od = chip_only[0::2], chip_only[1::2]
    sent = 0
    g.wait_ge(T.sem.qb1, 1)
    sent += _send(g, T, topo, core, hb[1], "bq", b0 + HB, b1, ev, "bc1_%d" % i)
    g.wait_ge(T.sem.qa0, 1)
    sent += _send(g, T, topo, core, rc[0], "aq", WA * own[0], WA * (own[0] + 1), od, "acod0")
    g.wait_ge(T.sem.qb0, 1)
    g.wait_ge(T.sem.qa1, 1)
    sent += _fused(g, T, topo, core, [(c_far, "bq", b0, b0 + HB, off, "bc0_%d" % i),
                                      (rc[1], "aq", WA * own[1], WA * (own[1] + 1), ev, "acod1"),
                                      (hb[0], "bq", b0, b0 + HB, od, "bc0_%d" % i)])
    sent += _fused(g, T, topo, core, [(c_far, "bp", b0, b1, off, "bpln%d" % i),
                                      (rp, "ap", WA * TA * j, WA * TA * (j + 1), ev, "apln"),
                                      (hp, "bp", b0, b1, od, "bpln%d" % i)])
    for name, c0, c1, sem, n_in in (("bq", f0, f0 + HB, "bc0_%d" % far, n_off), ("bp", f0, f1, "bpln%d" % far, n_off),
                                    ("bq", f0 + HB, f1, "bc1_%d" % far, n_rel)):
        g.wait_ge(T.sem[sem], n_in)
        sent += _send(g, T, topo, core, c_near, name, c0, c1, off, sem)

    when = {s: max(late[s], 2 if s in theirs else 0) for s in range(GR)}
    t = g.tensor
    t.wait_ge(T.sem.qa0, 1)
    t.wait_ge(T.sem.qa1, 1)
    t.wait_ge(T.sem.qb0, 1)
    t.wait_ge(T.sem.qb1, 1)
    for n, s in enumerate(sorted(range(GR), key=lambda s: when[s])):
        if s in theirs:
            t.wait_ge(T.sem.apln, n_rel)
            t.wait_ge(T.sem["acod%d" % theirs.index(s)], n_rel)
        for h in range(2):
            if s != i:
                t.wait_ge(T.sem["bc%d_%d" % (h, s)], n_rel if s == near or (s == far and h == 1) else n_off)
                t.wait_ge(T.sem["bpln%d" % s], n_rel if s == near else n_off)
            c0 = WB * s + HB * h
            t.matmul_mx(T.ps[:, BANK * h:BANK * h + HB], T.aq[:, WA * s:WA * (s + 1)], T.ap[:, WA * s:WA * (s + 1)],
                        T.bq[:, c0:c0 + HB], T.bp[:, c0:c0 + HB],
                        n == 0, n == GR - 1).then_inc(T.sem["mm%d" % h], 1)

    for h, q in enumerate((g.sync, g.scalar)):
        g.vector.wait_ge(T.sem["mm%d" % h], GR)
        g.vector.tensor_copy(T.yo[:, HB * h:HB * (h + 1)],
                             T.ps[:, BANK * h:BANK * h + HB]).then_inc(T.sem["cp%d" % h], 1)
        q.wait_ge(T.sem["cp%d" % h], 1)
        q.dma_start(T.y[:, HB * h:HB * (h + 1)], T.yo[:, HB * h:HB * (h + 1)]).then_inc(T.sem["st%d" % h], 16)
        q.wait_ge(T.sem["st%d" % h], 16)
    g.wait_ge(T.sem.sent, sent)


def rank_program(g, core, T, topo):
    job = _plan(T, topo).get(core)
    if job is None:
        return
    if job[0] == "relay":
        _relay(g, core, T, topo, job)
    else:
        _rank(g, core, T, topo, job)
